import numpy as np, ml_dtypes
CORES = [113,118,241,246]
N = 4
BF = ml_dtypes.bfloat16
def gentries(a):
    return np.ascontiguousarray(a.reshape(8, 16, -1).transpose(0, 2, 1)).reshape(8, -1)
def gtable(e):
    e = np.asarray(e); return np.ascontiguousarray(e.reshape(8, -1, 16).transpose(0, 2, 1)).reshape(128, -1).astype(np.int32)
W, L, P, T = 4096, 192, 16, 7
def place(z, e, kap):
    return ((z * (2 * e + 1)[..., None] >> 5) + z + kap) & (W - 1)
def parts(rng):
    low = rng.random((N, 8, 1, W)) < rng.choice(np.array([0.01, 0.03, 0.06, 0.15, 0.5]), (N, 8, 1, 1))
    x = np.where(low, rng.integers(0, 256, (N, 8, 16, W)), rng.integers(64, 256, (N, 8, 16, W)))
    c = rng.integers(0, W, (N, 8, L, 16)); o = rng.integers(0, W, (N, 8, L, P))
    d = np.where(rng.random((N, 8, 1, L)) < 0.5, rng.integers(1, 49, (N, 8, 16, L)), rng.integers(1, 256, (N, 8, 16, L)))
    return x, c, o, d, rng.integers(0, 16, (N, 8, 16, 1))
def pack(x, c, o, d, w):
    return {"xt": np.ascontiguousarray(x.reshape(N, 128, W)).astype(np.float32).astype(BF), "pk": np.stack([gtable(a.reshape(8, -1)) for a in c]), "po": np.stack([gtable(a.reshape(8, -1)) for a in o]),
            "dm": np.ascontiguousarray(d.reshape(N, 128, L)).astype(np.int32), "wt": np.ascontiguousarray(w.reshape(N, 128, 1)).astype(np.int32)}
def setup_inputs(rng):
    return pack(*parts(rng))
def setup_inputs_ties(rng):
    x, c, o, d, w = parts(rng)
    v = rng.integers(8, 200, (N, 8, 16, 1))
    x = v + np.where(rng.random((N, 8, 1, W)) < 0.75, rng.integers(-1, 2, (N, 8, 1, W)), rng.integers(-1, 2, (N, 8, 16, W)))
    d = v + rng.integers(-1, 2, (N, 8, 16, L))
    few = rng.integers(0, W, 8); few[0] = 0; few[7] = W - 1
    c[:, 1::2] = few[rng.integers(0, 8, (N, 4, L, 16))]; o[:, 1::2] = few[rng.integers(0, 8, (N, 4, L, P))]
    return pack(x, c, o, d, w)
def setup_inputs_corners(rng):
    x, c, o, d, w = parts(rng)
    d = rng.choice(np.array([1, 2, 4, 5, 6, 8, 9, 10, 128, 246, 247, 248, 251, 252, 255]), (N, 8, 16, L))
    d[:, :, :, :8] = 1; d[:, :, :, L - 8:] = 255
    x[:, 0] = x[:, 0, :, :1]
    c[:, 1] = c[:, 1, :, :1]; o[:, 1] = o[:, 1, :, :1]
    o[:, 2] = np.concatenate([c[:, 2, :, ::-1]] * (P // 16), axis=2)
    w[:, 3] = 0; w[:, 4] = 15; w[:, 5] = 0; w[:, 5, 15] = rng.integers(1, 16, (N, 1))
    x[:, 6] = 255 * rng.integers(0, 2, (N, 1, W))
    x[:, 7] = rng.integers(0, 256, (N, 16, W)); c[:, 7] = (W - 1) * rng.integers(0, 2, (N, L, 16)); o[:, 7] = (W - 1) * rng.integers(0, 2, (N, L, P))
    q = int(rng.integers(0, N)); x[q] = x[q, :, :, :1]
    return pack(x, c, o, d, w)
def setup_inputs_ends(rng):
    kind = rng.integers(0, 4, (N, 8, 1, W)); hole = rng.integers(0, 16, (N, 8, 1, W))
    x = np.where(kind == 0, 0, np.where(kind == 1, 1, np.where(kind == 2, rng.integers(0, 2, (N, 8, 16, W)), np.arange(16).reshape(16, 1) != hole)))
    w = rng.integers(0, 2, (N, 8, 16, 1)); w[:, 6] = 0; w[:, 7] = 1; w = 15 * w
    kd = rng.integers(0, 4, (N, 8, 1, L)); d = np.where(kd == 0, 0, np.where(kd == 1, 1, rng.integers(0, 2, (N, 8, 16, L))))
    d[:, :, :, L - 1] = 1; d[:, :, :, L - 2] = 0; d = 1 + 254 * d
    c = (W - 1) * rng.integers(0, 2, (N, 8, L, 16)); o = (W - 1) * rng.integers(0, 2, (N, 8, L, P))
    c[:, :, L - 2:] = 0; c[:, :, L - 2:, 15] = W - 1; c[:, :, L - 1, 2] = W - 1
    o[:, :, L - 2:] = W - 1; o[:, :, L - 2:, P - 1] = 0; o[:, :, L - 1, 1] = 0
    c[0, :, :, 7] = W - 1; o[0, :, :, P - 1] = 0; c[0, 3, 5] = 0
    c[N - 1, :, :, 15] = W - 1; o[N - 1, :, :, P - 1] = 0
    m = rng.random((8, L, 1)) < 0.5; c[1] = np.where(m, 0, W - 1); o[1] = np.where(m, o[1], W - 1)
    e = np.add.reduce(w * d, axis=2) & 1023
    p = place(np.full((N, 8, L, 1), W - 1), e, 0)[..., 0]
    tail = int(np.argmax(place(np.arange(W)[None, :], np.zeros(1, np.int64), 0)[0]))
    for q in (0, 1, N - 1):
        for g in range(8): x[q, g][:, p[q, g]] = 1
        x[q, :, :, 0] = 0
    for q in (0, N - 1):
        c[q, 6, L - 2:, 15] = tail; x[q, 6, :, W - 1] = 1
    return pack(255 * x, c, o, d, w)
def setup_inputs_lull(rng):
    x, c, o, d, w = parts(rng)
    q = int(rng.integers(0, N)); p = (q - 1) % N
    x[q] = np.maximum(x[q], 1); x[:, :, :, :32] = 255; x[p, :, :, :32] = 0; x[q, :, :, :32] = 0
    c[p] = 0; o[q, :, :, P - 2:] = 0; o[q] = rng.permuted(o[q], axis=2)
    still = rng.permutation(8 * L)[:int(rng.integers(1, 32))]; c[q, still // L, still % L] = 0
    return pack(x, c, o, d, w)
def setup_inputs_spread(rng):
    x = np.minimum((np.exp2(8 * rng.random((N, 8, 1, W))) * (0.5 + 0.5 * rng.random((N, 8, 16, W)))).astype(np.int64), 255) * (rng.random((N, 8, 1, W)) > 0.0625)
    c = np.minimum((W * rng.random((N, 8, L, 16)) ** 4).astype(np.int64), W - 1); o = np.minimum((W * rng.random((N, 8, L, P)) ** 4).astype(np.int64), W - 1)
    d = np.minimum(np.maximum(np.exp2(8 * rng.random((N, 8, 16, L))).astype(np.int64), 1), 255)
    w = rng.integers(0, 16, (N, 8, 16, 1)) * (rng.random((N, 8, 16, 1)) < 0.4)
    return pack(x, c, o, d, w)
def check_inputs(d):
    bad = []
    for k, lo, hi in (("xt", 0, 255), ("pk", 0, W - 1), ("po", 0, W - 1), ("dm", 1, 255), ("wt", 0, 15)):
        v = np.asarray(d[k]).astype(np.float64)
        if not np.all((v >= lo) & (v <= hi) & (v == np.floor(v))): bad.append("range of " + k)
    return bad
def picks(x, z, e, kap):
    return np.take(x, place(z, e, kap) + (W * np.arange(8 * N)).reshape(N, 8, 1, 1), axis=0)
def reference(xt, pk, po, dm, wt):
    x = np.ascontiguousarray(xt.astype(np.float32).astype(np.int32).reshape(8 * N, 16, W).transpose(0, 2, 1)).reshape(-1, 16)
    c = np.stack([gentries(a) for a in pk]).astype(np.int64).reshape(N, 8, L, 16)
    o = np.stack([gentries(a) for a in po]).astype(np.int64).reshape(N, 8, L, P)
    D = np.ascontiguousarray(dm.astype(np.int32).reshape(N, 8, 16, L).transpose(0, 1, 3, 2))
    w = wt.astype(np.int32).reshape(N, 8, 1, 16)
    kap = np.zeros((N, 1, 1, 1), np.int64); left = []
    for t in range(T):
        if t > 0: c = np.roll(c, 1, axis=0)
        e = (np.add.reduce(w * D, axis=3) & 1023).astype(np.int64)
        a = picks(x, c, e, kap); b = picks(x, o, e, kap)
        if t >= N:
            m = left[t - N]; y = picks(x, m, e, kap); gone = (m != c)[..., None]
            up = np.max(np.where(gone, -1, a), axis=3) >= np.max(np.where(gone, y, -1), axis=3)
            D = np.minimum(np.maximum(np.where(up, D + 8, D - 8), 1), 255)
        sa = np.add.reduce(np.minimum(a, D[:, :, :, None, :]), axis=4); sb = np.add.reduce(np.minimum(b, D[:, :, :, None, :]), axis=4)
        k = np.argmax(sa, axis=3)[..., None]; j = np.argmin(sb, axis=3)[..., None]
        swap = np.take_along_axis(sa, k, 3) > np.take_along_axis(sb, j, 3)
        ck = np.take_along_axis(c, k, 3); oj = np.take_along_axis(o, j, 3)
        np.put_along_axis(c, k, np.where(swap, oj, ck), 3); np.put_along_axis(o, j, np.where(swap, ck, oj), 3)
        xk = np.take_along_axis(a, k[..., None], 3)[:, :, :, 0]
        D = np.where(swap & (xk >= D), np.maximum(D - 4, 1), D)
        kap = np.add.reduce(swap.reshape(N, -1).astype(np.int64), axis=1).reshape(N, 1, 1, 1) & 31
        left.append(c)
    return {"yc": np.stack([gtable(v.reshape(8, -1)) for v in c]).astype(np.float32), "yo": np.stack([gtable(v.reshape(8, -1)) for v in o]).astype(np.float32),
            "yd": np.ascontiguousarray(D.transpose(0, 1, 3, 2)).reshape(N, 128, L).astype(np.float32)}

from concourse.bass import DstId, RemoteDMATransfer
from concourse.mybir import AluOpType, AxisListType, ActivationFunctionType

NV = 7
A_ = AluOpType
F_ = ActivationFunctionType
TAB = 16
WEND = TAB + 4096 + 32
BIG = -100000.0
VA, VDX = 2, 11


def _sb(dtype, *names, w=192):
    return {nm: ("sbuf", [128, w], dtype) for nm in names}


SCRATCH = {"dx": ("sbuf", [128, 12, 256], "bfloat16"), "rrow": ("sbuf", [1, 128], "bfloat16"),
           "c16": ("sbuf", [1, 192], "bfloat16"), "c3k": ("sbuf", [1, 16], "bfloat16"), "cff": ("sbuf", [1, 80], "bfloat16")}
SCRATCH.update(_sb("bfloat16", "xtw", w=WEND))
SCRATCH.update(_sb("bfloat16", "xo", "mo", "xc", "xa", "sa", w=3072))
SCRATCH.update(_sb("bfloat16", "mc", w=3088))
SCRATCH.update(_sb("bfloat16", "E", "NE", "WE", w=2048))
SCRATCH.update(_sb("bfloat16", "idn", "nid", "id4", "id16", "neg", w=128))
SCRATCH.update(_sb("bfloat16", "bd8", w=8))
SCRATCH.update(_sb("bfloat16", "ones", "rst", "D0", "D1", "D2", "Dt", "gn", "ind", "yb0", "yb1", "yb2", "up"))
SCRATCH.update(_sb("int32", "pki", "poi", "dmi", "pi", "pf", "ci", "cf", "mi", "mf", "sO"))
SCRATCH.update(_sb("uint16", "offo", "offc", "offa"))
SCRATCH.update(_sb("float32", "O0", "O1", "am", "kO", "kC", "OHO", "wO", "so", "Q", "sP", "OHP", "ds", "OO",
                   "ydf", "ycf", "yof"))
SCRATCH.update(_sb("float32", "cv1", "cv2", "cv3", "cv4", w=384))
SCRATCH.update(_sb("int32", "wti", "kq", w=1))
SCRATCH.update(_sb("float32", "wtf", "K", "kc", w=1))
SCRATCH.update(_sb("int32", "iP", "iC", "irow", "igp", "ich", "it0", "it1", "it2", "it3", "it4", w=24))
SCRATCH.update(_sb("uint16", "dupi", "dupo", w=24))
SCRATCH.update(_sb("uint16", "pick", "picko", "rep", "rep15", "aoff", w=12))
SCRATCH.update(_sb("int32", "ei", "eu", "hiO", "eff", "lo", w=16))
SCRATCH.update(_sb("float32", "vp", "thr", w=16))
SCRATCH.update(_sb("uint16", "offs", w=16))
SCRATCH.update(_sb("bfloat16", "sw", w=16))
SCRATCH.update(_sb("float32", "nn", w=72))
SCRATCH.update(_sb("float32", "ev", "evs", "ym", w=36))
SCRATCH.update(_sb("int32", "yq", "yf", w=36))
SCRATCH.update(_sb("uint16", "yoff", w=36))
SCRATCH.update(_sb("float32", "cin", "cout", w=192 * NV))
SCRATCH.update(_sb("float32", "rec", w=24 * (NV - 1)))
SCRATCH.update(_sb("float32", "rin", w=72 * NV))
PSUM = ("pd0", "pd1", "pkO", "pkA", "pkB", "pM1", "pM2", "pZ")
SCRATCH.update({nm: ("psum", [128, 512], "float32") for nm in PSUM})
SEMAPHORES = (["sv", "ss", "sp", "sg", "ls", "l_po", "l_dm", "l_pk", "l_wt", "l_xt", "s_yc", "s_yo", "s_yd"]
              + ["arr%d" % t for t in range(1, NV)] + [nm + str(t) for t in range(4, NV) for nm in ("ra", "rb")])


def rank_program(g, core, T, topo):
    rank = T.rank_of(core)
    if rank is None:
        return
    n = len(T.cores)
    queue = {"v": g.vector, "s": g.scalar, "p": g.tensor, "g": g, "y": g.sync}
    own = {"v": "sv", "s": "ss", "p": "sp", "g": "sg"}
    count = {"sv": 0, "ss": 0, "sp": 0, "sg": 0}
    known = {q: {} for q in queue}
    snap = {}
    last_w, readers = {}, {}

    def need(q, sem, val):
        if known[q].get(sem, 0) >= val:
            return
        queue[q].wait_ge(T.sem[sem], val)
        known[q][sem] = val
        for k2, v2 in snap.get((sem, val), {}).items():
            if known[q].get(k2, 0) < v2:
                known[q][k2] = v2

    def order(q, reads, writes):
        deps = {}

        def add(tok, skip_own=False):
            for sm, c in tok.items():
                if skip_own and sm == own.get(q):
                    continue
                if deps.get(sm, 0) < c:
                    deps[sm] = c
        for b in reads:
            add(last_w.get(b, {}))
            if b in PSUM:
                add(readers.get(b, {}), True)
        for b in writes:
            add(last_w.get(b, {}), q == "p")
            add(readers.get(b, {}), True)
        for sm in sorted(deps):
            need(q, sm, deps[sm])

    def note(tok_sem, tok_val, reads, writes):
        for b in writes:
            last_w[b] = {tok_sem: tok_val}
            readers[b] = {}
        for b in reads:
            readers.setdefault(b, {})[tok_sem] = tok_val

    def op(q, fn, reads, writes):
        order(q, reads, writes)
        sem = own[q]
        fn().then_inc(T.sem[sem], 1)
        count[sem] += 1
        snap[(sem, count[sem])] = dict(known[q])
        note(sem, count[sem], reads, writes)

    def dma(q, out, in_, sem, reads, writes):
        order(q, reads, writes)
        queue[q].dma_start(out, in_).then_inc(T.sem[sem], 16)
        snap[(sem, 16)] = dict(known[q])
        note(sem, 16, reads, writes)

    def arrived(buf, sem, val):
        last_w[buf] = {sem: val}
        readers[buf] = {}

    v, s, pe = g.vector, g.scalar, g.tensor
    width = {"cin": 192, "cout": 192, "rec": 24, "rin": 72}

    def X(name):
        base = name.rstrip("0123456789")
        if base not in width:
            return T[name][:]
        w = width[base]
        i = int(name[len(base):])
        return T[base][:, w * i:w * i + w]

    def V(fn, r, w):
        op("v", fn, r, w)

    def copy_s(out, in_, r, w, f=F_.Copy):
        op("s", lambda: s.activation(out, in_, f), r, w)

    def copy_v(out, in_, r, w):
        V(lambda: v.tensor_copy(out, in_), r, w)

    def fill(ap, c, w):
        V(lambda: v.memset(ap, c), [], w)

    def tt(out, a, b, o, r, w):
        V(lambda: v.tensor_tensor(out, a, b, o), r, w)

    def ts(out, a, s1, o0, r, w):
        V(lambda: v.tensor_scalar(out, a, s1, None, o0), r, w)

    def ts2(out, a, s1, s2, o0, o1, r, w):
        V(lambda: v.tensor_scalar(out, a, s1, s2, o0, o1), r, w)

    def scan(out, d0, d1, o1, r, w):
        V(lambda: v.tensor_tensor_scan(out, d0, d1, 0.0, A_.mult, o1), r, w)

    def mm(out, lhsT, rhs, st, sp, r, w):
        op("p", lambda: pe.matmul(out, lhsT, rhs, st, sp), r, w)

    def blk(nm, c0, c1):
        return ["%s%d" % (nm, c) for c in range(c0, c1)]

    dma("y", T.dmi[:], T.dm[:], "l_dm", [], ["dmi"])
    dma("y", T.poi[:], T.po[:], "l_po", [], ["poi"])
    dma("y", T.wti[:], T.wt[:], "l_wt", [], ["wti"])
    dma("s", T.xtw[:, TAB:TAB + 4096], T.xt[:], "l_xt", [], ["xtw"])
    dma("y", T.pki[:], T.pk[:], "l_pk", [], ["pki"])
    fill(T.bd8[:], 4096.0, ["bd8"])
    fill(T.ones[:], 1.0, ["ones"])
    fill(T.E[:], 0.0, ["E"])
    op("g", lambda: g.affine_select(T.bd8[:], T.bd8[:], [[-16, 8]], A_.is_ge, 0.0, 0, 1), ["bd8"], ["bd8"])
    op("g", lambda: g.affine_select(T.bd8[:], T.bd8[:], [[16, 8]], A_.is_ge, 0.0, 15, -1), ["bd8"], ["bd8"])
    op("g", lambda: g.iota(T.iP[:], [[0, 24]], 0, 1), [], ["iP"])
    op("g", lambda: g.iota(T.iC[:], [[1, 24]], 0, 0), [], ["iC"])
    op("g", lambda: g.affine_select(T.idn[:], T.ones[:, 0:128], [[-1, 128]], A_.is_equal, 0.0, 0, 1), ["ones"], ["idn"])
    op("g", lambda: g.iota(T.rrow[:], [[0, 8], [1, 16]], 0, 0, allow_small_or_imprecise_dtypes=True), [], ["rrow"])
    op("g", lambda: g.iota(T.c16[:], [[16, 192]], 0, 0, allow_small_or_imprecise_dtypes=True), [], ["c16"])
    for r in range(16):
        copy_s(T.E[:, r * 129:(r + 1) * 128:16], T.bd8[:], ["bd8", "E"], ["E%d" % r])
    EA = ["E"] + blk("E", 0, 16)
    ts(T.irow[:], T.iP[:], 15, A_.bitwise_and, ["iP"], ["irow"])
    ts(T.ich[:], T.iC[:], 1, A_.logical_shift_right, ["iC"], ["ich"])
    ts2(T.igp[:], T.iP[:], 4, 1, A_.logical_shift_right, A_.bitwise_and, ["iP"], ["igp"])
    ts(T.it0[:], T.ich[:], 16, A_.mult, ["ich"], ["it0"])
    copy_v(T.D0[:], T.dmi[:], ["dmi"], ["D0"])
    tt(T.it1[:], T.it0[:], T.irow[:], A_.add, ["it0", "irow"], ["it1"])
    ts(T.igp[:], T.igp[:], 16, A_.mult, ["igp"], ["igp"])
    copy_v(T.dupi[:], T.it1[:], ["it1"], ["dupi"])
    ts2(T.it2[:, 0:12], T.iC[:, 0:12], 32, 15, A_.mult, A_.add, ["iC"], ["it2"])
    tt(T.it3[:, 0:12], T.igp[:, 0:12], T.irow[:, 0:12], A_.subtract, ["igp", "irow"], ["it3"])
    copy_v(T.rep[:], T.iC[:, 0:12], ["iC"], ["rep"])
    tt(T.it2[:, 0:12], T.it2[:, 0:12], T.it3[:, 0:12], A_.add, ["it2", "it3"], ["it2"])
    ts(T.wtf[:], T.wti[:], 1.0 / 2048, A_.mult, ["wti"], ["wtf"])
    copy_v(T.pick[:], T.it2[:, 0:12], ["it2"], ["pick"])

    def seat_in(src, dst, a, b):
        copy_v(T[a][:], T[src][:].indirect(T.dupi[:]), [src, "dupi"], [a])
        V(lambda: v.transpose(T[b][:], T[a][:]), [a], [b])
        copy_v(X(dst), T[b][:].indirect(T.pick[:]), [b, "pick"], [dst])

    def seat_out(src, dst, a, b, out, sem, q, cp):
        cp(T[a][:], X(src).indirect(T.dupo[:]), [src, "dupo"], [a])
        V(lambda: v.transpose(T[b][:], T[a][:]), [a], [b])
        cp(T[dst][:], T[b][:].indirect(T.picko[:]), [b, "picko"], [dst])
        dma(q, out[:], T[dst][:], sem, [dst], [])

    seat_in("poi", "O0", "cv1", "cv2")
    ts(T.WE[:], T.E[:], T.wtf[:, 0:1], A_.mult, EA + ["wtf"], ["WE"])
    fill(T.K[:], 0.0, ["K"])
    ts(T.nid[:], T.idn[:], -1.0, A_.mult, ["idn"], ["nid"])
    fill(T.c3k[:], 3072.0, ["c3k"])
    fill(T.cff[:], 4096.0 * 4080, ["cff"])
    fill(T.cff[:, 68:72], 0.0, ["cff"])

    def constants_1():
        ts(T.NE[:], T.E[:], -1.0, A_.mult, EA, ["NE"])
        fill(T.mc[:, 3072:3088], 512.0, ["mc_end"])
        fill(T.Dt[:, 128:192], 0.0, ["Dt0"])
        ts(T.id4[:], T.idn[:], -4.0, A_.mult, ["idn"], ["id4"])
        fill(T.rst[:], 1.0, ["rst"])
        fill(T.rst[:, 0:192:16], 0.0, ["rst"])
        ts2(T.it4[:, 0:12], T.iC[:, 0:12], 16, 15, A_.mult, A_.add, ["iC"], ["it4"])
        copy_v(T.rep15[:], T.it4[:, 0:12], ["it4"], ["rep15"])

    def constants_2():
        fill(T.xtw[:, 0:TAB], -1.0, ["xt_m1"])
        fill(T.neg[:], -0.0625, ["neg"])
        ts(T.id16[:], T.idn[:], 16.0, A_.mult, ["idn"], ["id16"])
        ts2(T.it2[:, 0:12], T.iC[:, 0:12], 256, 240, A_.mult, A_.add, ["iC"], ["it2"])
        tt(T.it2[:, 0:12], T.it2[:, 0:12], T.irow[:, 0:12], A_.add, ["it2", "irow"], ["it2"])
        copy_v(T.aoff[:], T.it2[:, 0:12], ["it2"], ["aoff"])

    def constants_3():
        ts(T.it1[:], T.it0[:], 15, A_.add, ["it0"], ["it1"])
        tt(T.it1[:], T.it1[:], T.irow[:], A_.subtract, ["it1", "irow"], ["it1"])
        copy_v(T.dupo[:], T.it1[:], ["it1"], ["dupo"])
        ts(T.it4[:, 0:12], T.iC[:, 0:12], 32, A_.mult, ["iC"], ["it4"])
        tt(T.it4[:, 0:12], T.it4[:, 0:12], T.irow[:, 0:12], A_.add, ["it4", "irow"], ["it4"])
        tt(T.it4[:, 0:12], T.it4[:, 0:12], T.igp[:, 0:12], A_.add, ["it4", "igp"], ["it4"])
        copy_v(T.picko[:], T.it4[:, 0:12], ["it4"], ["picko"])

    win = T.xtw[:, TAB:WEND]
    winm = T.xtw[:, 0:WEND]
    XT = ["xtw", "xt_wrap"]
    XTM = ["xtw", "xt_wrap", "xt_m1"]
    DX = blk("dx", 0, 16)

    def E(r):
        return T.E[:, r * 128:(r + 1) * 128]

    def emit_e(dn):
        for r in range(16):
            mm(T.pM2[:, 0:12], T.WE[:, r * 128:(r + 1) * 128], T[dn][:, r:192:16], r == 0, r == 15, ["WE", dn], ["pM2"])

    def emit_v():
        copy_v(T.ei[:, 0:12], T.pM2[:, 0:12], ["pM2"], ["ei"])
        ts(T.eu[:, 0:12], T.ei[:, 0:12], 2047, A_.bitwise_and, ["ei"], ["eu"])
        ts(T.vp[:, 0:12], T.eu[:, 0:12], 33.0, A_.add, ["eu"], ["vp"])

    def columns(cards, a, b):
        tt(T[a][:], T.vp[:, 0:12].indirect(T.rep[:]), X(cards), A_.mult, ["vp", "rep", cards], [a])
        ts2(T[b][:], T[a][:], 5, 4095, A_.arith_shift_right, A_.bitwise_and, [a], [b])

    def emit_list(cards, a, b, off):
        columns(cards, a, b)
        ts(T[off][:], T[b][:], T.K[:, 0:1], A_.add, [b, "K"], [off])

    def emit_dx(dn, onv):
        for k in range(16):
            (copy_v if k in onv else copy_s)(T.dx[:, :, 16 * k:16 * k + 16], T[dn][:], [dn], ["dx%d" % k])

    def emit_sd(dn):
        mm(T.pkO[:, 192:204], T.ones[0:1, 0:128], T.c3k[0:1, 0:12], True, False, ["ones", "c3k"], ["pkO"])
        mm(T.pkO[:, 192:204], T.ones[0:1, 0:128], T.cff[0:1, 64:76], False, False, ["ones", "cff"], ["pkO"])
        for r in range(16):
            mm(T.pkO[:, 196:200], E(r), T[dn][:, 64 + r:128:16], False, r == 15, ["E%d" % r, dn], ["pkO"])

    def gather(onv, dst, off, c0, c1, w=None):
        o = T[dst][:, 256 * c0:256 * c1]
        i = (w or win).indirect(T[off][:, 16 * c0:16 * c1])
        (copy_v if onv else copy_s)(o, i, (XTM if w is not None else XT) + [off], blk(dst, c0, c1))

    def fused(dst, off, c0, c1):
        for c in range(c0, c1):
            tt(T[dst][:, 256 * c:256 * c + 256], win.indirect(T[off][:, 16 * c:16 * c + 16]), T.dx[:, c, :], A_.min,
               XT + [off] + DX, ["%s%d" % (dst, c)])

    def minus_x(j, src):
        b = "pd%d" % (j % 2)
        mm(T[b][:], T.nid[:], T[src][:, 512 * j:512 * j + 512], True, False, ["nid"] + blk(src, 2 * j, 2 * j + 2), [b])

    def plus_d(j, dst):
        b = "pd%d" % (j % 2)
        mm(T[b][:, 0:256], T.idn[:], T.dx[:, 2 * j, :], False, False, ["idn"] + DX, [b])
        mm(T[b][:, 256:512], T.idn[:], T.dx[:, 2 * j + 1, :], False, True, ["idn"] + DX, [b])
        copy_s(T[dst][:, 512 * j:512 * j + 512], T[b][:], [b], blk(dst, 2 * j, 2 * j + 2), F_.Relu)

    def pair(j, src, dst):
        minus_x(j, src)
        plus_d(j, dst)

    def bias(bank, lo, hi, ff):
        mm(T[bank][:, 0:hi - lo], T.ones[0:1, 0:128], T.c16[0:1, lo:hi], True, False, ["ones", "c16"], [bank])
        mm(T[bank][:, 0:hi - lo], T.rrow[0:1, :], T.ones[0:1, 0:hi - lo], False, False, ["ones", "rrow"], [bank])
        if ff:
            mm(T[bank][:, 0:ff], T.ones[0:1, 0:128], T.cff[0:1, 0:ff], False, False, ["ones", "cff"], [bank])

    def score(bank, src, c0, at, neg, final):
        for r in range(16):
            mm(T[bank][:, at:at + 64], T.NE[:, r * 128:(r + 1) * 128] if neg else E(r),
               T[src][:, 256 * c0 + r:256 * c0 + 1024:16], False, final and r == 15,
               ["NE" if neg else "E%d" % r] + blk(src, c0, c0 + 4), [bank])

    def send_pack(t):
        dst = T.cores[(rank + 1) % n]
        rid, pid = topo.addr(dst, core)
        need("g", *list(last_w["cout%d" % t].items())[0])
        eng = topo.engines(core, dst)[:8]
        g.remote_dma(X("cin%d" % (t + 1)), X("cout%d" % t), T.sem["arr%d" % (t + 1)], T.sem.ls, pid, rid,
                     sum(1 << e for e in eng))
        return len(eng)

    def send_rec(q):
        need("g", *list(last_w["rec%d" % q].items())[0])
        trs = []
        for d in (1, 2, 3):
            t = q + d
            if t < 4 or t >= NV:
                continue
            dst = T.cores[(rank + d) % n]
            rid, pid = topo.addr(dst, core)
            eng = topo.engines(core, dst)[2 * len(trs):2 * len(trs) + 2]
            b = 72 * t + 24 * (q - (t - 3))
            trs.append(RemoteDMATransfer(dst_ids=[DstId(rid=rid, pnc=pid)], dma_engine_mask=sum(1 << e for e in eng),
                                         remote_sem=T.sem[("rb%d" if d == 1 else "ra%d") % t], srcs=[X("rec%d" % q)],
                                         dsts=[T.rin[:, b:b + 24]]))
        if trs:
            g.remote_dma_fused(trs, local_sem=T.sem.ls)
        return 2 * len(trs)

    left = 0
    dcur, ocur = "D0", "O0"
    emit_e("D0")
    emit_v()
    emit_dx("D0", ())
    copy_s(T.xtw[:, TAB + 4096:WEND], T.xtw[:, TAB:TAB + 32], ["xtw"], ["xt_wrap"])
    for t in range(NV):
        back = t >= 4
        last = t == NV - 1
        c_in, c_out, mback = "cin%d" % t, "cout%d" % t, "cout%d" % (t - 4)
        onx = "O1" if t % 2 == 0 else "O0"
        emit_list(ocur, "pi", "pf", "offo")
        gather(False, "xo", "offo", 4, 6)
        copy_s(T.pZ[:, 0:192], X(ocur), [ocur], ["pZ"])
        if back:
            copy_s(T.pZ[:, 192:384], X(mback), [mback], ["pZ"])
        gather(False, "xo", "offo", 6, 8)
        if not back:
            emit_sd(dcur)
            pair(2, "xo", "mo")
            if t == 0:
                constants_1()
                seat_in("pki", "cin0", "cv3", "cv4")
            fused("mo", "offo", 0, 4)
            gather(False, "xo", "offo", 8, 10)
            pair(3, "xo", "mo")
            gather(False, "xo", "offo", 10, 12)
            if t == 1:
                constants_2()
            if t == 2:
                constants_3()
            if t > 0:
                arrived(c_in, "arr%d" % t, 8)
            emit_list(c_in, "ci", "cf", "offc")
            bias("pkO", 0, 192, 64)
            score("pkO", "mo", 0, 0, True, False)
            pair(4, "xo", "mo")
            score("pkO", "mo", 4, 64, False, False)
            pair(5, "xo", "mo")
            gather(False, "xc", "offc", 8, 10)
            fused("mc", "offc", 0, 4)
            bias("pkA", 0, 128, 0)
            score("pkA", "mc", 0, 0, False, False)
            score("pkO", "mo", 8, 128, False, True)
            gather(False, "xc", "offc", 10, 12)
            copy_s(T.kO[:], T.pkO[:, 0:192], ["pkO"], ["kO"])
            pair(4, "xc", "mc")
            fused("mc", "offc", 4, 8)
            pair(5, "xc", "mc")
        else:
            gather(False, "xo", "offo", 8, 12)
            P = [T.rin[:, 72 * t + 24 * i:72 * t + 24 * i + 12] for i in range(3)]
            C = [T.rin[:, 72 * t + 24 * i + 12:72 * t + 24 * i + 24] for i in range(3)]
            arrived("old", "ra%d" % t, 4)
            arrived("new", "rb%d" % t, 2)
            arrived(c_in, "arr%d" % t, 8)

            def first(i, r):
                tt(T.yq[:, 12 * i:12 * i + 12], T.vp[:, 0:12], C[i], A_.mult, ["vp", r], ["yq%d" % i])
            columns(mback, "mi", "mf")
            ts2(T.nn[:, 0:48], T.rin[:, 72 * t:72 * t + 48], 3072.0, BIG, A_.is_ge, A_.mult, ["old"], ["nna"])
            tt(T.ev[:, 0:12], P[0], P[1], A_.is_equal, ["old"], ["ev0"])
            first(0, "old")
            first(1, "old")
            tt(T.gn[:], X(c_in), T.pZ[:, 192:384], A_.not_equal, [c_in, "pZ"], ["gn"])
            ts(T.pM2[:, 128:320], T.gn[:], BIG, A_.mult, ["gn"], ["pM2"])
            tt(T.am[:], T.mf[:], T.pM2[:, 128:320], A_.add, ["mf", "pM2"], ["am"])
            ts2(T.offa[:], T.am[:], T.K[:, 0:1], float(TAB), A_.add, A_.add, ["am", "K"], ["offa"])
            va = 12 - VA
            for c in range(0, va, 3):
                gather(False, "xa", "offa", c, min(c + 3, va), winm)
            emit_list(c_in, "ci", "cf", "offc")
            ts2(T.nn[:, 48:72], T.rin[:, 72 * t + 48:72 * t + 72], 3072.0, BIG, A_.is_ge, A_.mult, ["new"], ["nnb"])
            tt(T.ev[:, 12:24], P[0], P[2], A_.is_equal, ["old", "new"], ["ev1"])
            tt(T.ev[:, 24:36], P[1], P[2], A_.is_equal, ["old", "new"], ["ev2"])
            first(2, "new")
            ts(T.evs[:], T.ev[:], BIG, A_.mult, blk("ev", 0, 3), ["evs"])
            ts2(T.yf[:], T.yq[:], 5, 4095, A_.arith_shift_right, A_.bitwise_and, blk("yq", 0, 3), ["yf"])
            for i in range(3):
                tt(T.ym[:, 12 * i:12 * i + 12], T.yf[:, 12 * i:12 * i + 12], T.nn[:, 24 * i:24 * i + 12], A_.add,
                   ["yf", "nna" if i < 2 else "nnb"], ["ym%d" % i])
            tt(T.ym[:, 12:36], T.ym[:, 12:36], T.evs[:, 0:24], A_.add, ["ym1", "ym2", "evs"], ["ym1", "ym2"])
            tt(T.ym[:, 24:36], T.ym[:, 24:36], T.evs[:, 24:36], A_.add, ["ym2", "evs"], ["ym2"])
            ts2(T.yoff[:], T.ym[:], T.K[:, 0:1], float(TAB), A_.add, A_.add, blk("ym", 0, 3) + ["K"], ["yoff"])
            if VA:
                gather(True, "xa", "offa", va, 12, winm)
            copy_v(T.yb0[:], winm.indirect(T.yoff[:, 0:12]), XTM + ["yoff"], ["yb0"])
            tt(T.yb1[:], winm.indirect(T.yoff[:, 12:24]), T.yb0[:], A_.max, XTM + ["yoff", "yb0"], ["yb1"])
            tt(T.yb2[:], winm.indirect(T.yoff[:, 24:36]), T.yb1[:], A_.max, XTM + ["yoff", "yb1"], ["yb2"])
            gather(False, "xc", "offc", 8, 12)
            mm(T.pM1[:, 0:192], T.neg[:], T.ones[:], True, False, ["neg", "ones"], ["pM1"])
            mm(T.pM1[:, 0:192], T.idn[:], T[dcur][:], False, False, ["idn", dcur], ["pM1"])
            minus_x(2, "xo")
            minus_x(3, "xo")
            for r in range(16):
                scan(T.sa[:, r:3072:16], T.rst[:], T.xa[:, r:3072:16], A_.max, ["rst"] + blk("xa", 0, 12), ["sa%d" % r])
            tt(T.up[:], T.sa[:].indirect(T.aoff[:]), T.yb2[:], A_.is_ge, blk("sa", 0, 16) + ["aoff", "yb2"], ["up"])
            mm(T.pM1[:, 0:192], T.id16[:], T.up[:], False, True, ["id16", "up"], ["pM1"])
            ts2(T.D2[:], T.pM1[:, 0:192], 1.0, 255.0, A_.max, A_.min, ["pM1"], ["D2"])
            dcur = "D2"
            emit_sd(dcur)
            emit_dx(dcur, range(VDX))
            fused("mo", "offo", 0, 4)
            plus_d(2, "mo")
            plus_d(3, "mo")
            pair(4, "xo", "mo")
            bias("pkO", 0, 192, 64)
            score("pkO", "mo", 0, 0, True, False)
            pair(5, "xo", "mo")
            pair(4, "xc", "mc")
            score("pkO", "mo", 4, 64, False, False)
            fused("mc", "offc", 0, 4)
            score("pkO", "mo", 8, 128, False, True)
            pair(5, "xc", "mc")
            copy_s(T.kO[:], T.pkO[:, 0:192], ["pkO"], ["kO"])
            bias("pkA", 0, 128, 0)
            score("pkA", "mc", 0, 0, False, False)
            fused("mc", "offc", 4, 8)
        score("pkA", "mc", 4, 64, False, True)
        copy_s(T.kC[:, 0:128], T.pkA[:, 0:128], ["pkA"], ["kCa"])
        copy_s(T.Dt[:, 0:128], T[dcur][:, 0:128], [dcur], ["Dt"])
        bias("pkB", 128, 192, 64)
        score("pkB", "mc", 8, 0, True, True)
        mm(T.pM1[:, 0:192], T.idn[:], T[dcur][:], True, False, ["idn", dcur], ["pM1"])
        scan(T.sO[:], T.rst[:], T.kO[:], A_.max, ["rst", "kO"], ["sO"])
        ts(T.hiO[:, 0:12], T.sO[:, 15:192:16], 0xFFF000, A_.bitwise_and, ["sO"], ["hiO"])
        tt(T.OHO[:], T.sO[:].indirect(T.rep15[:]), T.kO[:], A_.is_equal, ["sO", "rep15", "kO"], ["OHO"])
        tt(T.thr[:, 0:12], T.pkO[:, 192:204], T.hiO[:, 0:12], A_.subtract, ["pkO", "hiO"], ["thr"])
        tt(T.wO[:], T.OHO[:], T.pZ[:, 0:192], A_.mult, ["OHO", "pZ"], ["wO"])
        scan(T.so[:], T.rst[:], T.wO[:], A_.add, ["rst", "wO"], ["so"])
        tt(T.Q[:], T.so[:].indirect(T.rep15[:]), X(c_in), A_.subtract, ["so", "rep15", c_in], ["Q"])
        copy_s(T.pZ[:, 192:384], T.Q[:], ["Q"], ["pZ"])
        scan(T.sP[:, 0:128], T.rst[:, 0:128], T.kC[:, 0:128], A_.max, ["rst", "kCa"], ["sPa"])
        scan(T.sP[:, 128:192], T.rst[:, 128:192], T.pkB[:, 0:64], A_.max, ["rst", "pkB"], ["sPb"])
        copy_s(T.kC[:, 128:192], T.pkB[:, 0:64], ["pkB"], ["kCb"])
        tt(T.eff[:, 0:12], T.sP[:, 15:192:16], T.thr[:, 0:12], A_.max, ["sPa", "sPb", "thr"], ["eff"])
        ts(T.lo[:, 0:12], T.eff[:, 0:12], 4095, A_.bitwise_and, ["eff"], ["lo"])
        if not last:
            tt(T.sw[:, 0:12], T.eff[:, 0:12], T.thr[:, 0:12], A_.is_gt, ["eff", "thr"], ["sw"])
            mm(T.pM2[:, 16:28], T.ones[:, 0:128], T.sw[:, 0:12], True, True, ["ones", "sw"], ["pM2"])
        copy_v(T.offs[:, 0:12], T.lo[:, 0:12], ["lo"], ["offs"])
        tt(T.ind[:], T.mc[:].indirect(T.offs[:, 0:12]), T.Dt[:], A_.is_equal,
           blk("mc", 0, 12) + ["mc_end", "offs", "Dt", "Dt0"], ["ind"])
        mm(T.pM1[:, 0:192], T.id4[:], T.ind[:], False, True, ["id4", "ind"], ["pM1"])
        tt(T.OHP[:], T.eff[:, 0:12].indirect(T.rep[:]), T.kC[:], A_.is_equal, ["eff", "rep", "kCa", "kCb"], ["OHP"])

        def pack_out():
            tt(T.pkA[:, 192:384], T.OHP[:], T.pZ[:, 192:384], A_.mult, ["OHP", "pZ"], ["pkA"])
            tt(X(c_out), X(c_in), T.pkA[:, 192:384], A_.add, [c_in, "pkA"], [c_out])
            return 0 if last else send_pack(t)
        if t >= 3:
            left += pack_out()
        if last:
            ts(T.ydf[:], T.pM1[:, 0:192], 1.0, A_.max, ["pM1"], ["ydf"])
            dma("y", T.yd[:], T.ydf[:], "s_yd", ["ydf"], [])
        else:
            nxt = "D1" if t % 2 == 0 else "D0"
            ts(T[nxt][:], T.pM1[:, 0:192], 1.0, A_.max, ["pM1"], [nxt])
            dcur = nxt
            V(lambda: v.tensor_reduce(T.kc[:], T.pM2[:, 16:28], AxisListType.X, A_.add), ["pM2"], ["kc"])
            emit_e(dcur)
            if t + 1 < 4:
                emit_dx(dcur, ())
        if t < 3:
            left += pack_out()
        scan(T.ds[:], T.rst[:], T.pkA[:, 192:384], A_.add, ["rst", "pkA"], ["ds"])
        if not last:
            ts2(T.kq[:], T.kc[:], 1.0 / 32, -0.5 + 1.0 / 64, A_.mult, A_.add, ["kc"], ["kq"])
        tt(T.OO[:], T.ds[:].indirect(T.rep15[:]), T.OHO[:], A_.mult, ["ds", "rep15", "OHO"], ["OO"])
        if not last:
            ts2(T.K[:], T.kq[:], -32.0, T.kc[:, 0:1], A_.mult, A_.add, ["kq", "kc"], ["K"])
        tt(X(onx), T.pZ[:, 0:192], T.OO[:], A_.subtract, ["pZ", "OO"], [onx])
        if not last:
            emit_v()
        if last:
            seat_out(c_out, "ycf", "cv1", "cv2", T.yc, "s_yc", "y", copy_s)
            seat_out(onx, "yof", "cv3", "cv4", T.yo, "s_yo", "y", copy_v)
        if 1 <= t < NV - 1:
            rc = "rec%d" % t
            copy_v(T.rec[:, 24 * t:24 * t + 12], T.lo[:, 0:12], ["lo"], [rc])
            tt(T.rec[:, 24 * t + 12:24 * t + 24], T.so[:, 15:192:16], T.ds[:, 15:192:16], A_.subtract, ["so", "ds"], [rc])
            left += send_rec(t)
        ocur = onx
    for sem in ("sv", "ss", "sp", "sg"):
        need("g", sem, count[sem])
    for sem in ("l_po", "l_dm", "l_pk", "l_wt", "l_xt", "s_yc", "s_yo", "s_yd"):
        need("g", sem, 16)
    g.wait_ge(T.sem.ls, left)
